import numpy as np
import ml_dtypes


def mxq(x, axis, fmt="e4m3"):
    dtype, down = {"e4m3": (ml_dtypes.float8_e4m3fn, 7), "e5m2": (ml_dtypes.float8_e5m2, 14)}[fmt]
    v = np.moveaxis(np.asarray(x, np.float32).astype(ml_dtypes.bfloat16).astype(np.float64), axis, -1)
    blocks = v.reshape(v.shape[:-1] + (-1, 32))
    amax = np.abs(blocks).max(-1, keepdims=True)
    byte = np.maximum(np.where(amax > 0, np.frexp(amax)[1] - 1 + 127, 0) - down, 1)
    scale = np.exp2(byte - 127.0)
    codes = (blocks / scale).astype(np.float32).astype(dtype).astype(np.float64)
    return np.moveaxis((codes * scale).reshape(v.shape), -1, axis)


WIDE = False


def mx_kscale(k):
    if not WIDE:
        return np.ones(k)
    levels = np.array([10, -10, 5, -5, 0])
    if k % 512:
        return np.exp2(np.random.permutation(np.resize(levels, k // 32))).repeat(32)
    a = np.empty((k // 512, 16))
    for p in range(k // 512):
        a[p, :8] = np.random.permutation(np.resize(levels, 8))
        for g in range(8):
            far = levels[np.abs(levels - a[p, g]) >= 10]
            a[p, g + 8] = far[np.random.randint(len(far))]
    return np.exp2(a.ravel()).repeat(32)


def f64(x):
    return np.asarray(x).astype(np.float64)


def striped8(idx):
    return np.concatenate([x.reshape(-1, 16).T for x in idx]).astype(np.uint16)


def runs(offs, k):
    lists = np.stack([offs[16 * r : 16 * r + 16].T.reshape(-1) for r in range(8)]).astype(np.int64)
    return lists[np.arange(k) % 512 // 64]


def pack_weight(w):
    k, n = w.shape
    w = f64(np.asarray(w, np.float32).astype(ml_dtypes.bfloat16)).reshape(k // 32, 32, n)
    amax = np.abs(w).max(1)
    byte = np.clip(np.where(amax > 0, np.frexp(amax)[1] - 1 + 127 - 7, 1), 1, 254)
    scaled = (w * np.exp2(127.0 - byte)[:, None, :]).reshape(k, n).astype(np.float32)
    words = np.ascontiguousarray(scaled.reshape(k // 512, 128, 4, n).transpose(0, 1, 3, 2)).astype(ml_dtypes.float8_e4m3fn).view(np.uint8)
    return words, np.ascontiguousarray(byte.astype(np.uint8).reshape(k // 512, 16, n))


def unpack_weight(words, scales):
    g, p, n, _ = words.shape
    vals = np.ascontiguousarray(words).view(ml_dtypes.float8_e4m3fn).astype(np.float64) * np.repeat(np.exp2(scales.astype(np.float64) - 127.0), 8, axis=1)[..., None]
    return vals.transpose(0, 1, 3, 2).reshape(g * 512, n)


K, T, S, G, H, W = 512, 1024, 512, 2048, 512, 256


def setup_inputs():
    n = np.random.standard_normal
    s = mx_kscale(K)[:, None]
    packed_xT = pack_weight(n((K, T)) * s)
    packed_dT = pack_weight(n((K, G)) / s)
    perm = np.stack([np.random.permutation(S) for _ in range(8)])
    return {
        "x_words": packed_xT[0],
        "x_scales": packed_xT[1],
        "d_words": packed_dT[0],
        "d_scales": packed_dT[1],
        "gs": (np.random.uniform(0.5, 1.5, (K, 1)) * s).astype(np.float32),
        "offs": striped8(np.random.randint(0, T, (8, S))),
        "k1": striped8(np.random.randint(0, G, (8, H))),
        "k2": striped8(np.random.randint(0, G, (8, H))),
        "n1": striped8(perm[:, :W]),
        "n2": striped8(perm[:, W:]),
        "n3": striped8(np.stack([np.random.permutation(S) for _ in range(8)])),
    }


def reference(x_words, x_scales, d_words, d_scales, gs, offs, k1, k2, n1, n2, n3):
    d_k2 = unpack_weight(d_words, d_scales)[np.arange(K)[:, None], runs(k2, K)]
    d_k1 = unpack_weight(d_words, d_scales)[np.arange(K)[:, None], runs(k1, K)]
    xq = unpack_weight(x_words, x_scales)[np.arange(K)[:, None], runs(offs, K)]
    h = 0.0625 * (d_k1.T @ xq)
    z = f64(gs) * h
    h2 = 0.0625 * ((d_k2.T @ mxq(z, 0, "e4m3")))
    pa = h2[np.arange(H)[:, None], runs(n1, H)]
    pb = h2[np.arange(H)[:, None], runs(n2, H)]
    ra = np.maximum(pa, pb)
    ds = h2.copy()
    ds[np.arange(H)[:, None], runs(n1, H)] = ra
    return ds - (ds[np.arange(H)[:, None], runs(n3, H)])

@@ -1,0 +1,177 @@
+from contextlib import ExitStack
+
+import concourse.mybir as mybir
+
+K, T, S, G, H, W = 512, 1024, 512, 2048, 512, 256
+FLOPS = 2 * K * H * S + 2 * H * H * S
+
+F32 = mybir.dt.float32
+BF16 = mybir.dt.bfloat16
+I32 = mybir.dt.int32
+U32 = mybir.dt.uint32
+U16 = mybir.dt.uint16
+U8 = mybir.dt.uint8
+FP8X4 = mybir.dt.float8_e4m3fn_x4
+COPY = mybir.ActivationFunctionType.Copy
+ALU = mybir.AluOpType
+
+P = 128
+PACK = 4
+HALF = S // 2
+
+
+def tile_picked_hcodeifillm_none_p_kernel(tc, x_words, x_scales, d_words, d_scales, gs, offs, k1, k2, n1, n2, n3, out):
+    nc = tc.nc
+    with ExitStack() as ctx:
+        keep = ctx.enter_context(tc.tile_pool(name="keep", bufs=1))
+        psum = ctx.enter_context(tc.psum_pool(name="psum", bufs=1))
+
+        def load_list(name, dram):
+            t = keep.tile([P, dram.shape[1]], U16, name=name)
+            nc.sync.dma_start(t[:], dram)
+            return t
+
+        def load_scale_table(name, dram, width):
+            t = keep.tile([P, width], U8, name=name, align_bytes=64)
+            rows = dram[0].bitcast(I32).unsqueeze(1).to_broadcast([16, 8, width // 4])
+            nc.sync.dma_start(t[:].bitcast(I32), rows)
+            return t
+
+        def load_word_table(name, dram, width):
+            t = keep.tile([P, width], U32, name=name, align_bytes=64)
+            nc.sync.dma_start(t[:].bitcast(I32), dram[0].rearrange("p c r -> p (c r)").bitcast(I32))
+            return t
+
+        def gather(name, table, lst, dtype):
+            t = keep.tile([P, S], dtype, name=name, align_bytes=64)
+            nc.vector.tensor_copy(t[:], table[:].indirect(lst[:]))
+            return t
+
+        def place_rows(plane):
+            for i in range(1, 4):
+                nc.sync.dma_start(plane[i:P:32, :].bitcast(I32), plane[8 * i:P:32, :].bitcast(I32))
+
+        offs_sb = load_list("offs_sb", offs)
+        xs_tab = load_scale_table("xs_tab", x_scales, T)
+        k1_sb = load_list("k1_sb", k1)
+        ds_tab = load_scale_table("ds_tab", d_scales, G)
+        xw_tab = load_word_table("xw_tab", x_words, T)
+        dw_tab = load_word_table("dw_tab", d_words, G)
+        gs_sb = keep.tile([P, PACK], F32, name="gs_sb")
+        nc.sync.dma_start(gs_sb[:], gs.rearrange("(p t) o -> p (t o)", t=PACK))
+        k2_sb = load_list("k2_sb", k2)
+        n1_sb = load_list("n1_sb", n1)
+        n2_sb = load_list("n2_sb", n2)
+        n3_sb = load_list("n3_sb", n3)
+
+        gs16 = keep.tile([P, PACK], F32, name="gs16")
+        nc.scalar.activation(gs16[:], gs_sb[:], COPY, scale=0.0625)
+
+        xs_g = gather("xs_g", xs_tab, offs_sb, U8)
+        d1s_g = gather("d1s_g", ds_tab, k1_sb, U8)
+        plane1 = keep.tile([P, S + H], U8, name="plane1", align_bytes=64)
+        nc.vector.tensor_copy(plane1[:, :S].bitcast(I32), xs_g[:].bitcast(I32))
+        nc.vector.tensor_copy(
+            plane1[:, S:].rearrange("p (t c i) -> p c t i", t=PACK, i=16),
+            d1s_g[:].rearrange("p (c i t) -> p c t i", t=PACK, i=16),
+        )
+        place_rows(plane1)
+        xw_g = gather("xw_g", xw_tab, offs_sb, U32)
+        d1w_g = gather("d1w_g", dw_tab, k1_sb, U32)
+        d1w = keep.tile([P, H], U32, name="d1w", align_bytes=64)
+        nc.vector.tensor_copy(
+            d1w[:].rearrange("p (t c i) -> p c t i", t=PACK, i=4),
+            d1w_g[:].rearrange("p (c i t) -> p c t i", t=PACK, i=4),
+        )
+
+        zp = keep.tile([P, PACK, S], BF16, name="zp", align_bytes=64)
+        for t in range(PACK):
+            acc = psum.tile([P, S], F32, name="acc1", tag="bank%d" % t)
+            cols = slice(t * P, (t + 1) * P)
+            nc.tensor.matmul_mx(
+                out=acc[:], lhsT=d1w[:, cols].bitcast(FP8X4), lhsT_scale=plane1[:, S + t * P:S + (t + 1) * P],
+                rhs=xw_g[:].bitcast(FP8X4), rhs_scale=plane1[:, :S], start=True, stop=True,
+            )
+            nc.scalar.activation(zp[:, t, :], acc[:], COPY, scale=gs16[:, t:t + 1])
+
+        d2s_g = gather("d2s_g", ds_tab, k2_sb, U8)
+        plane2 = keep.tile([P, H], U8, name="plane2", align_bytes=64)
+        nc.vector.tensor_copy(
+            plane2[:].bitcast(I32).rearrange("p (t g m) -> p g t m", t=PACK, m=2),
+            d2s_g[:].bitcast(I32).rearrange("p (g t m) -> p g t m", t=PACK, m=2),
+        )
+        place_rows(plane2)
+        d2w_g = gather("d2w_g", dw_tab, k2_sb, U32)
+        d2w = keep.tile([P, H], U32, name="d2w", align_bytes=64)
+        nc.vector.tensor_copy(
+            d2w[:].rearrange("p (t g m) -> p g t m", t=PACK, m=8),
+            d2w_g[:].rearrange("p (g t m) -> p g t m", t=PACK, m=8),
+        )
+
+        zi = [keep.tile([P, HALF * PACK], BF16, name="zi%d" % h, align_bytes=64) for h in range(2)]
+        zw = [keep.tile([P, HALF], U32, name="zw%d" % h, align_bytes=64) for h in range(2)]
+        zs = [keep.tile([P, HALF], U8, name="zs%d" % h, align_bytes=64) for h in range(2)]
+        for h in range(2):
+            nc.vector.tensor_copy(
+                zi[h][:].rearrange("p (c i t) -> p c t i", t=PACK, i=4),
+                zp[:, :, h * HALF:(h + 1) * HALF].rearrange("p t (c i) -> p c t i", i=4),
+            )
+        for h in range(2):
+            nc.vector.quantize_mx(out=zw[h][:].bitcast(FP8X4), scales=zs[h][:], in_=zi[h][:])
+
+        h2 = [keep.tile([P, S], F32, name="h2_%d" % t) for t in range(PACK)]
+        pa = [keep.tile([P, W], F32, name="pa%d" % t) for t in range(PACK)]
+        pb = [keep.tile([P, W], F32, name="pb%d" % t) for t in range(PACK)]
+        ra = [keep.tile([P, W], F32, name="ra%d" % t) for t in range(PACK)]
+        far = [keep.tile([P, S], F32, name="far%d" % t) for t in range(PACK)]
+        res = [keep.tile([P, S], F32, name="res%d" % t) for t in range(PACK)]
+        out_rows = out.rearrange("(g t m) j -> t g m j", t=PACK, m=8)
+
+        def product(t):
+            cols = slice(t * P, (t + 1) * P)
+            if t == 0:
+                accs = [psum.tile([P, HALF], F32, name="acc2", tag="half%d" % h)[:] for h in range(2)]
+            else:
+                whole = psum.tile([P, S], F32, name="acc2", tag="bank%d" % t)
+                accs = [whole[:, h * HALF:(h + 1) * HALF] for h in range(2)]
+            for h in range(2):
+                nc.tensor.matmul_mx(
+                    out=accs[h], lhsT=d2w[:, cols].bitcast(FP8X4), lhsT_scale=plane2[:, cols],
+                    rhs=zw[h][:].bitcast(FP8X4), rhs_scale=zs[h][:], start=True, stop=True,
+                )
+                if t == 0:
+                    nc.scalar.activation(h2[t][:, h * HALF:(h + 1) * HALF], accs[h], COPY, scale=0.0625)
+            if t > 0:
+                nc.scalar.activation(h2[t][:], whole[:], COPY, scale=0.0625)
+
+        def fetch_pairs(t):
+            nc.scalar.activation(pa[t][:], h2[t][:].indirect(n1_sb[:]), COPY)
+            if t == 0:
+                nc.vector.tensor_copy(pb[t][:], h2[t][:].indirect(n2_sb[:]))
+            else:
+                nc.scalar.activation(pb[t][:], h2[t][:].indirect(n2_sb[:]), COPY)
+
+        def put_larger(t):
+            nc.vector.tensor_tensor(ra[t][:], pa[t][:], pb[t][:], ALU.max)
+            nc.vector.tensor_copy(h2[t][:].indirect(n1_sb[:]), ra[t][:])
+
+        def fetch_far(t):
+            for h in range(2):
+                dst = far[t][:, h * HALF:(h + 1) * HALF]
+                src = h2[t][:].indirect(n3_sb[:, h * 16:(h + 1) * 16])
+                if t == PACK - 1 and h == 1:
+                    nc.vector.tensor_copy(dst, src)
+                else:
+                    nc.scalar.activation(dst, src, COPY)
+
+        def finish(t):
+            nc.vector.tensor_tensor(res[t][:], h2[t][:], far[t][:], ALU.subtract)
+            nc.sync.dma_start(out_rows[t], res[t][:])
+
+        for t in range(PACK):
+            product(t)
+            fetch_pairs(t)
+            put_larger(t)
+        for t in range(PACK):
+            fetch_far(t)
+            finish(t)

@@ -42,24 +42,24 @@ def tile_picked_hcodeifillm_none_p_kernel(tc, x_words, x_scales, d_words, d_scal
             nc.sync.dma_start(t[:].bitcast(I32), dram[0].rearrange("p c r -> p (c r)").bitcast(I32))
             return t
 
-        def gather(name, table, lst, dtype):
-            t = keep.tile([P, S], dtype, name=name, align_bytes=64)
-            nc.vector.tensor_copy(t[:], table[:].indirect(lst[:]))
+        def gather(name, table, lst, dtype, tag=None):
+            t = keep.tile([P, lst.shape[1] * 16], dtype, name=name, tag=tag or name, align_bytes=64)
+            nc.vector.tensor_copy(t[:], table[:].indirect(lst))
             return t
 
         def place_rows(plane):
             for i in range(1, 4):
                 nc.sync.dma_start(plane[i:P:32, :].bitcast(I32), plane[8 * i:P:32, :].bitcast(I32))
 
-        offs_sb = load_list("offs_sb", offs)
         xs_tab = load_scale_table("xs_tab", x_scales, T)
-        k1_sb = load_list("k1_sb", k1)
+        offs_sb = load_list("offs_sb", offs)
         ds_tab = load_scale_table("ds_tab", d_scales, G)
-        xw_tab = load_word_table("xw_tab", x_words, T)
+        k1_sb = load_list("k1_sb", k1)
         dw_tab = load_word_table("dw_tab", d_words, G)
+        xw_tab = load_word_table("xw_tab", x_words, T)
+        k2_sb = load_list("k2_sb", k2)
         gs_sb = keep.tile([P, PACK], F32, name="gs_sb")
         nc.sync.dma_start(gs_sb[:], gs.rearrange("(p t) o -> p (t o)", t=PACK))
-        k2_sb = load_list("k2_sb", k2)
         n1_sb = load_list("n1_sb", n1)
         n2_sb = load_list("n2_sb", n2)
         n3_sb = load_list("n3_sb", n3)
@@ -67,8 +67,8 @@ def tile_picked_hcodeifillm_none_p_kernel(tc, x_words, x_scales, d_words, d_scal
         gs16 = keep.tile([P, PACK], F32, name="gs16")
         nc.scalar.activation(gs16[:], gs_sb[:], COPY, scale=0.0625)
 
-        xs_g = gather("xs_g", xs_tab, offs_sb, U8)
-        d1s_g = gather("d1s_g", ds_tab, k1_sb, U8)
+        xs_g = gather("xs_g", xs_tab, offs_sb[:], U8)
+        d1s_g = gather("d1s_g", ds_tab, k1_sb[:], U8)
         plane1 = keep.tile([P, S + H], U8, name="plane1", align_bytes=64)
         nc.vector.tensor_copy(plane1[:, :S].bitcast(I32), xs_g[:].bitcast(I32))
         nc.vector.tensor_copy(
@@ -76,48 +76,53 @@ def tile_picked_hcodeifillm_none_p_kernel(tc, x_words, x_scales, d_words, d_scal
             d1s_g[:].rearrange("p (c i t) -> p c t i", t=PACK, i=16),
         )
         place_rows(plane1)
-        xw_g = gather("xw_g", xw_tab, offs_sb, U32)
-        d1w_g = gather("d1w_g", dw_tab, k1_sb, U32)
+        d1w_g = gather("d1w_g", dw_tab, k1_sb[:], U32)
         d1w = keep.tile([P, H], U32, name="d1w", align_bytes=64)
         nc.vector.tensor_copy(
             d1w[:].rearrange("p (t c i) -> p c t i", t=PACK, i=4),
             d1w_g[:].rearrange("p (c i t) -> p c t i", t=PACK, i=4),
         )
 
-        zp = keep.tile([P, PACK, S], BF16, name="zp", align_bytes=64)
-        for t in range(PACK):
-            acc = psum.tile([P, S], F32, name="acc1", tag="bank%d" % t)
-            cols = slice(t * P, (t + 1) * P)
-            nc.tensor.matmul_mx(
-                out=acc[:], lhsT=d1w[:, cols].bitcast(FP8X4), lhsT_scale=plane1[:, S + t * P:S + (t + 1) * P],
-                rhs=xw_g[:].bitcast(FP8X4), rhs_scale=plane1[:, :S], start=True, stop=True,
-            )
-            nc.scalar.activation(zp[:, t, :], acc[:], COPY, scale=gs16[:, t:t + 1])
+        xw_g = [gather("xw_g%d" % h, xw_tab, offs_sb[:, h * 16:(h + 1) * 16], U32) for h in range(2)]
 
-        d2s_g = gather("d2s_g", ds_tab, k2_sb, U8)
+        zp = [keep.tile([P, PACK, HALF], BF16, name="zp%d" % h, align_bytes=64) for h in range(2)]
+        for h in range(2):
+            for t in range(PACK):
+                acc = psum.tile([P, HALF], F32, name="acc1", tag="bank%d" % (PACK * h + t))
+                nc.tensor.matmul_mx(
+                    out=acc[:], lhsT=d1w[:, t * P:(t + 1) * P].bitcast(FP8X4),
+                    lhsT_scale=plane1[:, S + t * P:S + (t + 1) * P],
+                    rhs=xw_g[h][:].bitcast(FP8X4), rhs_scale=plane1[:, h * HALF:(h + 1) * HALF],
+                    start=True, stop=True,
+                )
+                nc.scalar.activation(zp[h][:, t, :], acc[:], COPY, scale=gs16[:, t:t + 1])
+
+        d2s_g = gather("d2s_g", ds_tab, k2_sb[:], U8, tag="d2_g1")
         plane2 = keep.tile([P, H], U8, name="plane2", align_bytes=64)
         nc.vector.tensor_copy(
             plane2[:].bitcast(I32).rearrange("p (t g m) -> p g t m", t=PACK, m=2),
             d2s_g[:].bitcast(I32).rearrange("p (g t m) -> p g t m", t=PACK, m=2),
         )
         place_rows(plane2)
-        d2w_g = gather("d2w_g", dw_tab, k2_sb, U32)
+        d2w_g = [gather("d2w_g%d" % h, dw_tab, k2_sb[:, h * 16:(h + 1) * 16], U32, tag="d2_g%d" % h) for h in range(2)]
         d2w = keep.tile([P, H], U32, name="d2w", align_bytes=64)
-        nc.vector.tensor_copy(
-            d2w[:].rearrange("p (t g m) -> p g t m", t=PACK, m=8),
-            d2w_g[:].rearrange("p (g t m) -> p g t m", t=PACK, m=8),
-        )
-
-        zi = [keep.tile([P, HALF * PACK], BF16, name="zi%d" % h, align_bytes=64) for h in range(2)]
-        zw = [keep.tile([P, HALF], U32, name="zw%d" % h, align_bytes=64) for h in range(2)]
-        zs = [keep.tile([P, HALF], U8, name="zs%d" % h, align_bytes=64) for h in range(2)]
         for h in range(2):
             nc.vector.tensor_copy(
-                zi[h][:].rearrange("p (c i t) -> p c t i", t=PACK, i=4),
-                zp[:, :, h * HALF:(h + 1) * HALF].rearrange("p t (c i) -> p c t i", i=4),
+                d2w[:].rearrange("p (t g m) -> p g t m", t=PACK, m=8)[:, 8 * h:8 * h + 8],
+                d2w_g[h][:].rearrange("p (g t m) -> p g t m", t=PACK, m=8),
             )
-        for h in range(2):
-            nc.vector.quantize_mx(out=zw[h][:].bitcast(FP8X4), scales=zs[h][:], in_=zi[h][:])
+
+        zi = [keep.tile([P, HALF * PACK], BF16, name="zi%d" % h, align_bytes=64) for h in range(2)]
+        zw = keep.tile([P, S], U32, name="zw", align_bytes=64)
+        zs = keep.tile([P, S], U8, name="zs", align_bytes=64)
+        for h, copy in ((1, nc.vector.tensor_copy), (0, nc.scalar.copy)):
+            copy(
+                zi[h][:].rearrange("p (c i t) -> p c t i", t=PACK, i=4),
+                zp[h][:].rearrange("p t (c i) -> p c t i", i=4),
+            )
+        for h in (1, 0):
+            cols = slice(h * HALF, (h + 1) * HALF)
+            nc.vector.quantize_mx(out=zw[:, cols].bitcast(FP8X4), scales=zs[:, cols], in_=zi[h][:])
 
         h2 = [keep.tile([P, S], F32, name="h2_%d" % t) for t in range(PACK)]
         pa = [keep.tile([P, W], F32, name="pa%d" % t) for t in range(PACK)]
@@ -127,51 +132,62 @@ def tile_picked_hcodeifillm_none_p_kernel(tc, x_words, x_scales, d_words, d_scal
         res = [keep.tile([P, S], F32, name="res%d" % t) for t in range(PACK)]
         out_rows = out.rearrange("(g t m) j -> t g m j", t=PACK, m=8)
 
-        def product(t):
-            cols = slice(t * P, (t + 1) * P)
-            if t == 0:
-                accs = [psum.tile([P, HALF], F32, name="acc2", tag="half%d" % h)[:] for h in range(2)]
+        def product(t, cols, bank, on_vector=False):
+            rows = slice(t * P, (t + 1) * P)
+            acc = psum.tile([P, cols.stop - cols.start], F32, name="acc2", tag="bank%d" % bank)
+            nc.tensor.matmul_mx(
+                out=acc[:], lhsT=d2w[:, rows].bitcast(FP8X4), lhsT_scale=plane2[:, rows],
+                rhs=zw[:, cols].bitcast(FP8X4), rhs_scale=zs[:, cols], start=True, stop=True,
+            )
+            if on_vector:
+                nc.vector.tensor_scalar(h2[t][:, cols], acc[:], 0.0625, None, ALU.mult)
             else:
-                whole = psum.tile([P, S], F32, name="acc2", tag="bank%d" % t)
-                accs = [whole[:, h * HALF:(h + 1) * HALF] for h in range(2)]
-            for h in range(2):
-                nc.tensor.matmul_mx(
-                    out=accs[h], lhsT=d2w[:, cols].bitcast(FP8X4), lhsT_scale=plane2[:, cols],
-                    rhs=zw[h][:].bitcast(FP8X4), rhs_scale=zs[h][:], start=True, stop=True,
-                )
-                if t == 0:
-                    nc.scalar.activation(h2[t][:, h * HALF:(h + 1) * HALF], accs[h], COPY, scale=0.0625)
-            if t > 0:
-                nc.scalar.activation(h2[t][:], whole[:], COPY, scale=0.0625)
+                nc.scalar.activation(h2[t][:, cols], acc[:], COPY, scale=0.0625)
 
-        def fetch_pairs(t):
-            nc.scalar.activation(pa[t][:], h2[t][:].indirect(n1_sb[:]), COPY)
-            if t == 0:
-                nc.vector.tensor_copy(pb[t][:], h2[t][:].indirect(n2_sb[:]))
-            else:
-                nc.scalar.activation(pb[t][:], h2[t][:].indirect(n2_sb[:]), COPY)
+        def fetch(dst, t, lst):
+            nc.scalar.activation(dst[t][:], h2[t][:].indirect(lst[:]), COPY)
 
-        def put_larger(t):
+        def larger(t):
             nc.vector.tensor_tensor(ra[t][:], pa[t][:], pb[t][:], ALU.max)
+
+        def put(t):
             nc.vector.tensor_copy(h2[t][:].indirect(n1_sb[:]), ra[t][:])
 
         def fetch_far(t):
             for h in range(2):
-                dst = far[t][:, h * HALF:(h + 1) * HALF]
-                src = h2[t][:].indirect(n3_sb[:, h * 16:(h + 1) * 16])
-                if t == PACK - 1 and h == 1:
-                    nc.vector.tensor_copy(dst, src)
-                else:
-                    nc.scalar.activation(dst, src, COPY)
+                nc.scalar.activation(
+                    far[t][:, h * HALF:(h + 1) * HALF], h2[t][:].indirect(n3_sb[:, h * 16:(h + 1) * 16]), COPY
+                )
 
         def finish(t):
-            nc.vector.tensor_tensor(res[t][:], h2[t][:], far[t][:], ALU.subtract)
-            nc.sync.dma_start(out_rows[t], res[t][:])
+            pieces = 2 if t == PACK - 1 else 1
+            width = S // pieces
+            for h in range(pieces):
+                cols = slice(h * width, (h + 1) * width)
+                nc.vector.tensor_tensor(res[t][:, cols], h2[t][:, cols], far[t][:, cols], ALU.subtract)
+                nc.sync.dma_start(out_rows[t][:, :, cols], res[t][:, cols])
 
-        for t in range(PACK):
-            product(t)
-            fetch_pairs(t)
-            put_larger(t)
+        left, right, both = slice(0, HALF), slice(HALF, S), slice(0, S)
+        product(0, right, 0)
+        product(0, left, 1, on_vector=True)
+        product(1, left, 2)
+        fetch(pa, 0, n1_sb)
+        nc.vector.tensor_copy(pb[0][:], h2[0][:].indirect(n2_sb[:]))
+        larger(0)
+        put(0)
+        product(1, right, 0, on_vector=True)
+        product(2, both, 1)
+        fetch(pa, 1, n1_sb)
+        fetch(pb, 1, n2_sb)
+        larger(1)
+        put(1)
+        product(3, both, 2)
+        for dst, lst in ((pa, n1_sb), (pb, n2_sb)):
+            for t in (2, 3):
+                fetch(dst, t, lst)
+        for step in (larger, put):
+            for t in (2, 3):
+                step(t)
         for t in range(PACK):
             fetch_far(t)
             finish(t)

@@ -55,13 +55,13 @@ def tile_picked_hcodeifillm_none_p_kernel(tc, x_words, x_scales, d_words, d_scal
         offs_sb = load_list("offs_sb", offs)
         ds_tab = load_scale_table("ds_tab", d_scales, G)
         k1_sb = load_list("k1_sb", k1)
+        n1_sb = load_list("n1_sb", n1)
+        n2_sb = load_list("n2_sb", n2)
         dw_tab = load_word_table("dw_tab", d_words, G)
         xw_tab = load_word_table("xw_tab", x_words, T)
         k2_sb = load_list("k2_sb", k2)
         gs_sb = keep.tile([P, PACK], F32, name="gs_sb")
         nc.sync.dma_start(gs_sb[:], gs.rearrange("(p t) o -> p (t o)", t=PACK))
-        n1_sb = load_list("n1_sb", n1)
-        n2_sb = load_list("n2_sb", n2)
         n3_sb = load_list("n3_sb", n3)
 
         gs16 = keep.tile([P, PACK], F32, name="gs16")
@@ -155,17 +155,22 @@ def tile_picked_hcodeifillm_none_p_kernel(tc, x_words, x_scales, d_words, d_scal
 
         def fetch_far(t):
             for h in range(2):
-                nc.scalar.activation(
-                    far[t][:, h * HALF:(h + 1) * HALF], h2[t][:].indirect(n3_sb[:, h * 16:(h + 1) * 16]), COPY
-                )
+                dst = far[t][:, h * HALF:(h + 1) * HALF]
+                src = h2[t][:].indirect(n3_sb[:, h * 16:(h + 1) * 16])
+                if t == PACK - 1 and h == 1:
+                    nc.vector.tensor_copy(dst, src)
+                else:
+                    nc.scalar.activation(dst, src, COPY)
 
         def finish(t):
-            pieces = 2 if t == PACK - 1 else 1
-            width = S // pieces
-            for h in range(pieces):
-                cols = slice(h * width, (h + 1) * width)
-                nc.vector.tensor_tensor(res[t][:, cols], h2[t][:, cols], far[t][:, cols], ALU.subtract)
-                nc.sync.dma_start(out_rows[t][:, :, cols], res[t][:, cols])
+            if t < PACK - 1:
+                nc.gpsimd.tensor_tensor(res[t][:], h2[t][:], far[t][:], ALU.subtract)
+                nc.sync.dma_start(out_rows[t], res[t][:])
+            else:
+                for h in (1, 0):
+                    cols = slice(h * HALF, (h + 1) * HALF)
+                    nc.vector.tensor_tensor(res[t][:, cols], h2[t][:, cols], far[t][:, cols], ALU.subtract)
+                    nc.sync.dma_start(out_rows[t][:, :, cols], res[t][:, cols])
 
         left, right, both = slice(0, HALF), slice(HALF, S), slice(0, S)
         product(0, right, 0)

@@ -170,7 +170,7 @@ def tile_picked_hcodeifillm_none_p_kernel(tc, x_words, x_scales, d_words, d_scal
                 for h in (1, 0):
                     cols = slice(h * HALF, (h + 1) * HALF)
                     nc.vector.tensor_tensor(res[t][:, cols], h2[t][:, cols], far[t][:, cols], ALU.subtract)
-                    nc.sync.dma_start(out_rows[t][:, :, cols], res[t][:, cols])
+                    nc.scalar.dma_start(out_rows[t][:, :, cols], res[t][:, cols])
 
         left, right, both = slice(0, HALF), slice(HALF, S), slice(0, S)
         product(0, right, 0)
@@ -180,13 +180,13 @@ def tile_picked_hcodeifillm_none_p_kernel(tc, x_words, x_scales, d_words, d_scal
         nc.vector.tensor_copy(pb[0][:], h2[0][:].indirect(n2_sb[:]))
         larger(0)
         put(0)
-        product(1, right, 0, on_vector=True)
-        product(2, both, 1)
+        product(1, right, 1, on_vector=True)
+        product(2, both, 2)
         fetch(pa, 1, n1_sb)
         fetch(pb, 1, n2_sb)
         larger(1)
         put(1)
-        product(3, both, 2)
+        product(3, both, 0)
         for dst, lst in ((pa, n1_sb), (pb, n2_sb)):
             for t in (2, 3):
                 fetch(dst, t, lst)

from contextlib import ExitStack

import concourse.mybir as mybir

K, T, S, G, H, W = 512, 1024, 512, 2048, 512, 256
FLOPS = 2 * K * H * S + 2 * H * H * S

F32 = mybir.dt.float32
BF16 = mybir.dt.bfloat16
I32 = mybir.dt.int32
U32 = mybir.dt.uint32
U16 = mybir.dt.uint16
U8 = mybir.dt.uint8
FP8X4 = mybir.dt.float8_e4m3fn_x4
COPY = mybir.ActivationFunctionType.Copy
ALU = mybir.AluOpType

P = 128
PACK = 4
HALF = S // 2


def tile_picked_hcodeifillm_none_p_kernel(tc, x_words, x_scales, d_words, d_scales, gs, offs, k1, k2, n1, n2, n3, out):
    nc = tc.nc
    with ExitStack() as ctx:
        keep = ctx.enter_context(tc.tile_pool(name="keep", bufs=1))
        psum = ctx.enter_context(tc.psum_pool(name="psum", bufs=1))

        def load_list(name, dram):
            t = keep.tile([P, dram.shape[1]], U16, name=name)
            nc.sync.dma_start(t[:], dram)
            return t

        def load_scale_table(name, dram, width):
            t = keep.tile([P, width], U8, name=name, align_bytes=64)
            rows = dram[0].bitcast(I32).unsqueeze(1).to_broadcast([16, 8, width // 4])
            nc.sync.dma_start(t[:].bitcast(I32), rows)
            return t

        def load_word_table(name, dram, width):
            t = keep.tile([P, width], U32, name=name, align_bytes=64)
            nc.sync.dma_start(t[:].bitcast(I32), dram[0].rearrange("p c r -> p (c r)").bitcast(I32))
            return t

        def gather(name, table, lst, dtype, tag=None):
            t = keep.tile([P, lst.shape[1] * 16], dtype, name=name, tag=tag or name, align_bytes=64)
            nc.vector.tensor_copy(t[:], table[:].indirect(lst))
            return t

        def place_rows(plane):
            for i in range(1, 4):
                nc.sync.dma_start(plane[i:P:32, :].bitcast(I32), plane[8 * i:P:32, :].bitcast(I32))

        xs_tab = load_scale_table("xs_tab", x_scales, T)
        offs_sb = load_list("offs_sb", offs)
        ds_tab = load_scale_table("ds_tab", d_scales, G)
        k1_sb = load_list("k1_sb", k1)
        n1_sb = load_list("n1_sb", n1)
        n2_sb = load_list("n2_sb", n2)
        dw_tab = load_word_table("dw_tab", d_words, G)
        xw_tab = load_word_table("xw_tab", x_words, T)
        k2_sb = load_list("k2_sb", k2)
        gs_sb = keep.tile([P, PACK], F32, name="gs_sb")
        nc.sync.dma_start(gs_sb[:], gs.rearrange("(p t) o -> p (t o)", t=PACK))
        n3_sb = load_list("n3_sb", n3)

        gs16 = keep.tile([P, PACK], F32, name="gs16")
        nc.scalar.activation(gs16[:], gs_sb[:], COPY, scale=0.0625)

        xs_g = gather("xs_g", xs_tab, offs_sb[:], U8)
        d1s_g = gather("d1s_g", ds_tab, k1_sb[:], U8)
        plane1 = keep.tile([P, S + H], U8, name="plane1", align_bytes=64)
        nc.vector.tensor_copy(plane1[:, :S].bitcast(I32), xs_g[:].bitcast(I32))
        nc.vector.tensor_copy(
            plane1[:, S:].rearrange("p (t c i) -> p c t i", t=PACK, i=16),
            d1s_g[:].rearrange("p (c i t) -> p c t i", t=PACK, i=16),
        )
        place_rows(plane1)
        d1w_g = gather("d1w_g", dw_tab, k1_sb[:], U32)
        d1w = keep.tile([P, H], U32, name="d1w", align_bytes=64)
        nc.vector.tensor_copy(
            d1w[:].rearrange("p (t c i) -> p c t i", t=PACK, i=4),
            d1w_g[:].rearrange("p (c i t) -> p c t i", t=PACK, i=4),
        )

        xw_g = [gather("xw_g%d" % h, xw_tab, offs_sb[:, h * 16:(h + 1) * 16], U32) for h in range(2)]

        zp = [keep.tile([P, PACK, HALF], BF16, name="zp%d" % h, align_bytes=64) for h in range(2)]
        for h in range(2):
            for t in range(PACK):
                acc = psum.tile([P, HALF], F32, name="acc1", tag="bank%d" % (PACK * h + t))
                nc.tensor.matmul_mx(
                    out=acc[:], lhsT=d1w[:, t * P:(t + 1) * P].bitcast(FP8X4),
                    lhsT_scale=plane1[:, S + t * P:S + (t + 1) * P],
                    rhs=xw_g[h][:].bitcast(FP8X4), rhs_scale=plane1[:, h * HALF:(h + 1) * HALF],
                    start=True, stop=True,
                )
                nc.scalar.activation(zp[h][:, t, :], acc[:], COPY, scale=gs16[:, t:t + 1])

        d2s_g = gather("d2s_g", ds_tab, k2_sb[:], U8, tag="d2_g1")
        plane2 = keep.tile([P, H], U8, name="plane2", align_bytes=64)
        nc.vector.tensor_copy(
            plane2[:].bitcast(I32).rearrange("p (t g m) -> p g t m", t=PACK, m=2),
            d2s_g[:].bitcast(I32).rearrange("p (g t m) -> p g t m", t=PACK, m=2),
        )
        place_rows(plane2)
        d2w_g = [gather("d2w_g%d" % h, dw_tab, k2_sb[:, h * 16:(h + 1) * 16], U32, tag="d2_g%d" % h) for h in range(2)]
        d2w = keep.tile([P, H], U32, name="d2w", align_bytes=64)
        for h in range(2):
            nc.vector.tensor_copy(
                d2w[:].rearrange("p (t g m) -> p g t m", t=PACK, m=8)[:, 8 * h:8 * h + 8],
                d2w_g[h][:].rearrange("p (g t m) -> p g t m", t=PACK, m=8),
            )

        zi = [keep.tile([P, HALF * PACK], BF16, name="zi%d" % h, align_bytes=64) for h in range(2)]
        zw = keep.tile([P, S], U32, name="zw", align_bytes=64)
        zs = keep.tile([P, S], U8, name="zs", align_bytes=64)
        for h, copy in ((1, nc.vector.tensor_copy), (0, nc.scalar.copy)):
            copy(
                zi[h][:].rearrange("p (c i t) -> p c t i", t=PACK, i=4),
                zp[h][:].rearrange("p t (c i) -> p c t i", i=4),
            )
        for h in (1, 0):
            cols = slice(h * HALF, (h + 1) * HALF)
            nc.vector.quantize_mx(out=zw[:, cols].bitcast(FP8X4), scales=zs[:, cols], in_=zi[h][:])

        h2 = [keep.tile([P, S], F32, name="h2_%d" % t) for t in range(PACK)]
        pa = [keep.tile([P, W], F32, name="pa%d" % t) for t in range(PACK)]
        pb = [keep.tile([P, W], F32, name="pb%d" % t) for t in range(PACK)]
        ra = [keep.tile([P, W], F32, name="ra%d" % t) for t in range(PACK)]
        far = [keep.tile([P, S], F32, name="far%d" % t) for t in range(PACK)]
        res = [keep.tile([P, S], F32, name="res%d" % t) for t in range(PACK)]
        out_rows = out.rearrange("(g t m) j -> t g m j", t=PACK, m=8)

        def product(t, cols, bank, on_vector=False):
            rows = slice(t * P, (t + 1) * P)
            acc = psum.tile([P, cols.stop - cols.start], F32, name="acc2", tag="bank%d" % bank)
            nc.tensor.matmul_mx(
                out=acc[:], lhsT=d2w[:, rows].bitcast(FP8X4), lhsT_scale=plane2[:, rows],
                rhs=zw[:, cols].bitcast(FP8X4), rhs_scale=zs[:, cols], start=True, stop=True,
            )
            if on_vector:
                nc.vector.tensor_scalar(h2[t][:, cols], acc[:], 0.0625, None, ALU.mult)
            else:
                nc.scalar.activation(h2[t][:, cols], acc[:], COPY, scale=0.0625)

        def fetch(dst, t, lst):
            nc.scalar.activation(dst[t][:], h2[t][:].indirect(lst[:]), COPY)

        def larger(t):
            nc.vector.tensor_tensor(ra[t][:], pa[t][:], pb[t][:], ALU.max)

        def put(t):
            nc.vector.tensor_copy(h2[t][:].indirect(n1_sb[:]), ra[t][:])

        def fetch_far(t):
            for h in range(2):
                dst = far[t][:, h * HALF:(h + 1) * HALF]
                src = h2[t][:].indirect(n3_sb[:, h * 16:(h + 1) * 16])
                if t == PACK - 1 and h == 1:
                    nc.vector.tensor_copy(dst, src)
                else:
                    nc.scalar.activation(dst, src, COPY)

        def finish(t):
            if t < PACK - 1:
                nc.gpsimd.tensor_tensor(res[t][:], h2[t][:], far[t][:], ALU.subtract)
                nc.sync.dma_start(out_rows[t], res[t][:])
            else:
                for h in (1, 0):
                    cols = slice(h * HALF, (h + 1) * HALF)
                    nc.vector.tensor_tensor(res[t][:, cols], h2[t][:, cols], far[t][:, cols], ALU.subtract)
                    nc.scalar.dma_start(out_rows[t][:, :, cols], res[t][:, cols])

        left, right, both = slice(0, HALF), slice(HALF, S), slice(0, S)
        product(0, right, 0)
        product(0, left, 1, on_vector=True)
        product(1, left, 2)
        fetch(pa, 0, n1_sb)
        nc.vector.tensor_copy(pb[0][:], h2[0][:].indirect(n2_sb[:]))
        larger(0)
        put(0)
        product(1, right, 1, on_vector=True)
        product(2, both, 2)
        fetch(pa, 1, n1_sb)
        fetch(pb, 1, n2_sb)
        larger(1)
        put(1)
        product(3, both, 0)
        for dst, lst in ((pa, n1_sb), (pb, n2_sb)):
            for t in (2, 3):
                fetch(dst, t, lst)
        for step in (larger, put):
            for t in (2, 3):
                step(t)
        for t in range(PACK):
            fetch_far(t)
            finish(t)
